import numpy as np
import ml_dtypes


def mxq(x, axis, fmt="e4m3"):
    dtype, down = {"e4m3": (ml_dtypes.float8_e4m3fn, 7), "e5m2": (ml_dtypes.float8_e5m2, 14)}[fmt]
    v = np.moveaxis(np.asarray(x, np.float32).astype(ml_dtypes.bfloat16).astype(np.float64), axis, -1)
    blocks = v.reshape(v.shape[:-1] + (-1, 32))
    amax = np.abs(blocks).max(-1, keepdims=True)
    byte = np.maximum(np.where(amax > 0, np.frexp(amax)[1] - 1 + 127, 0) - down, 1)
    scale = np.exp2(byte - 127.0)
    codes = (blocks / scale).astype(np.float32).astype(dtype).astype(np.float64)
    return np.moveaxis((codes * scale).reshape(v.shape), -1, axis)


WIDE = False


def mx_kscale(k):
    if not WIDE:
        return np.ones(k)
    levels = np.array([10, -10, 5, -5, 0])
    if k % 512:
        return np.exp2(np.random.permutation(np.resize(levels, k // 32))).repeat(32)
    a = np.empty((k // 512, 16))
    for p in range(k // 512):
        a[p, :8] = np.random.permutation(np.resize(levels, 8))
        for g in range(8):
            far = levels[np.abs(levels - a[p, g]) >= 10]
            a[p, g + 8] = far[np.random.randint(len(far))]
    return np.exp2(a.ravel()).repeat(32)


def f64(x):
    return np.asarray(x).astype(np.float64)


def striped(idx):
    return np.tile(idx.reshape(-1, 16).T, (8, 1)).astype(np.uint16)


def unstriped(offs):
    return offs[:16].T.reshape(-1).astype(np.int64)


E2M1 = np.array([0.0, 0.5, 1.0, 1.5, 2.0, 3.0, 4.0, 6.0, -0.0, -0.5, -1.0, -1.5, -2.0, -3.0, -4.0, -6.0])


def pack_weight(w, fmt):
    k, n = w.shape
    w = f64(np.asarray(w, np.float32).astype(ml_dtypes.bfloat16)).reshape(k // 32, 32, n)
    amax = np.abs(w).max(1)
    if fmt == "e4m3":
        byte = np.frexp(amax)[1] - 1 + 127 - 7
    else:
        mant, ex = np.frexp(amax / 6.0)
        byte = np.where(mant > 0.5, ex, ex - 1) + 127
    byte = np.clip(np.where(amax > 0, byte, 1), 1, 254)
    scaled = (w * np.exp2(127.0 - byte)[:, None, :]).reshape(k, n).astype(np.float32)
    by_word = np.ascontiguousarray(scaled.reshape(k // 512, 128, 4, n).transpose(0, 1, 3, 2))
    if fmt == "e4m3":
        words = by_word.astype(ml_dtypes.float8_e4m3fn).view(np.uint8)
    else:
        c = by_word.astype(ml_dtypes.float4_e2m1fn).view(np.uint8) & 0xF
        words = (c[..., 0::2] | (c[..., 1::2] << 4)).reshape(k // 512, 128, 2 * n)
    return np.ascontiguousarray(words), np.ascontiguousarray(byte.astype(np.uint8).reshape(k // 512, 16, n))


def unpack_weight(words, scales, fmt):
    g, _, n = scales.shape
    words = np.ascontiguousarray(words).reshape(g, 128, n, -1)
    if fmt == "e4m3":
        vals = words.view(ml_dtypes.float8_e4m3fn).astype(np.float64)
    else:
        nib = np.empty((g, 128, n, 4), np.uint8)
        nib[..., 0::2] = words & 0xF
        nib[..., 1::2] = words >> 4
        vals = E2M1[nib]
    vals = vals * np.repeat(np.exp2(scales.astype(np.float64) - 127.0), 8, axis=1)[..., None]
    return vals.transpose(0, 1, 3, 2).reshape(g * 512, n)


def gelu(v):
    return 0.5 * v * (1.0 + np.tanh(np.sqrt(2.0 / np.pi) * (v + 0.044715 * v**3)))


K, T, S, H, N, T2, P = 1024, 2048, 1024, 1024, 384, 2048, 1024


def setup_inputs():
    n = np.random.standard_normal
    s = mx_kscale(K)[:, None]
    u = mx_kscale(H)[:, None]
    tab_words, tab_scales = pack_weight(n((K, T)) * s, "e4m3")
    w4_words, w4_scales = pack_weight(n((H, N)) / np.sqrt(H) / u, "e2m1")
    return {
        "tab_words": tab_words,
        "tab_scales": tab_scales,
        "offs": striped(np.random.permutation(T)[:S]),
        "offs2": striped(np.random.permutation(T2)[:S]),
        "offs3": striped(np.random.permutation(T2)[:P]),
        "page0": (n((H, T2)) * u).astype(np.float32),
        "w1": (n((K, H)) / np.sqrt(K) / s * u.T).astype(np.float32),
        "w4_words": w4_words,
        "w4_scales": w4_scales,
        "w3": (n((K, N)) / np.sqrt(K) / s).astype(np.float32),
        "b": (0.7 * n(N)).astype(np.float32),
    }


def reference(tab_words, tab_scales, offs, offs2, offs3, page0, w1, w4_words, w4_scales, w3, b):
    v = unpack_weight(tab_words, tab_scales, "e4m3")[:, unstriped(offs)]
    h = mxq(f64(w1), 0, "e4m3").T @ v
    page = f64(page0).copy()
    l2 = unstriped(offs2)
    page[:, l2] = np.maximum(page[:, l2], h)
    x = page[:, unstriped(offs3)]
    w4 = unpack_weight(w4_words, w4_scales, "e2m1")
    y = w4.T @ mxq(x, 0, "e4m3")
    fresh = (mxq(f64(w3), 0, "e4m3").T @ v) + f64(b)[:, None]
    return np.maximum(y, fresh)

@@ -1,0 +1,278 @@
+from contextlib import ExitStack
+
+import concourse.mybir as mybir
+
+K, T, S, H, N, T2 = 1024, 2048, 1024, 1024, 384, 2048
+FLOPS = 2 * K * S * H + 2 * H * S * N + 2 * K * S * N
+
+F32 = mybir.dt.float32
+BF16 = mybir.dt.bfloat16
+I32 = mybir.dt.int32
+U32 = mybir.dt.uint32
+U16 = mybir.dt.uint16
+U8 = mybir.dt.uint8
+FP8X4 = mybir.dt.float8_e4m3fn_x4
+FP4X4 = mybir.dt.float4_e2m1fn_x4
+MAX = mybir.AluOpType.max
+IDENTITY = mybir.ActivationFunctionType.Identity
+
+P = 128
+PACK = 4
+K_PASS = P * PACK
+PASSES = 2
+BANK = 512
+N_TILES = N // P
+PAGE_TILES = H // P
+CHUNK = 256
+CHUNKS = S // CHUNK
+PER_COLUMN = 16
+
+
+def tile_list_defibrillator_battery_doubt_kernel(
+    tc, tab_words, tab_scales, offs, offs2, offs3, page0, w1, w4_words, w4_scales, w3, b, out
+):
+    nc = tc.nc
+    with ExitStack() as ctx:
+        keep = ctx.enter_context(tc.tile_pool(name="keep", bufs=1))
+        stage = ctx.enter_context(tc.tile_pool(name="stage", bufs=2))
+        psum = ctx.enter_context(tc.psum_pool(name="psum", bufs=1))
+
+        def bank(number, shape):
+            return psum.tile(shape, F32, name="bank%d" % number, tag="bank%d" % number)
+
+        def held(name, shape, dtype):
+            return keep.tile(shape, dtype, name=name, align_bytes=64)
+
+        list1 = keep.tile([P, S // PER_COLUMN], U16, name="list1")
+        list2 = keep.tile([P, S // PER_COLUMN], U16, name="list2")
+        list3 = keep.tile([P, S // PER_COLUMN], U16, name="list3")
+        tab_codes = [held("tab_codes%d" % a, [P, T], I32) for a in range(PASSES)]
+        tab_plane = held("tab_plane", [P, T], U8)
+        v_codes = [held("v_codes%d" % a, [P, S], U32) for a in range(PASSES)]
+        v_plane = held("v_plane", [P, S], U8)
+        pages = [held("page%d" % i, [P, T2], F32) for i in range(PAGE_TILES)]
+        w1_codes = {(a, g): held("w1_codes%d%d" % (a, g), [P, K_PASS], U32) for a in range(PASSES) for g in range(PASSES)}
+        w1_plane = {(a, g): held("w1_plane%d%d" % (a, g), [P, K_PASS], U8) for a in range(PASSES) for g in range(PASSES)}
+        w3_codes = [held("w3_codes%d" % a, [P, N], U32) for a in range(PASSES)]
+        w3_plane = [held("w3_plane%d" % a, [P, N], U8) for a in range(PASSES)]
+        w4_codes = held("w4_codes", [P, PASSES, 2 * N], U8)
+        w4_plane = held("w4_plane", [P, PASSES, N], U8)
+        bias = held("bias", [P, N_TILES], F32)
+        x_rows = [held("x_rows%d" % g, [P, PACK, S], BF16) for g in range(PASSES)]
+        x_grouped = [held("x_grouped%d" % g, [P, S, PACK], BF16) for g in range(PASSES)]
+        x_codes = [held("x_codes%d" % g, [P, S], U32) for g in range(PASSES)]
+        x_plane = [held("x_plane%d" % g, [P, S], U8) for g in range(PASSES)]
+        result = held("result", [P, CHUNKS, N_TILES, CHUNK], F32)
+
+        def load_tab_codes(a):
+            nc.sync.dma_start(out=tab_codes[a][:], in_=tab_words[a].rearrange("p t i -> p (t i)").bitcast(I32))
+
+        def load_page(i):
+            g, t = divmod(i, PACK)
+            rows = page0[g * K_PASS : (g + 1) * K_PASS, :].rearrange("(p t) c -> p t c", t=PACK)
+            nc.sync.dma_start(out=pages[i][:], in_=rows[:, t, :])
+
+        def load_weight(rows):
+            raw = stage.tile([P, PACK, rows.shape[1]], F32, name="raw", tag="raw", bufs=3)
+            nc.sync.dma_start(out=raw[:], in_=rows.rearrange("(p j) c -> p j c", j=PACK))
+            return raw
+
+        def load_w1(a, g):
+            return load_weight(w1[a * K_PASS : (a + 1) * K_PASS, g * K_PASS : (g + 1) * K_PASS])
+
+        def group_w1(raw):
+            grouped = stage.tile([P, PACK, P, PACK], BF16, name="grouped", tag="grouped", align_bytes=64)
+            nc.scalar.copy(
+                out=grouped[:].rearrange("p t m j -> p m j t"),
+                in_=raw[:].rearrange("p j (m t) -> p m j t", t=PACK),
+            )
+            return grouped
+
+        def quantize_w1(grouped, a, g):
+            nc.vector.quantize_mx(
+                out=w1_codes[a, g][:].bitcast(FP8X4),
+                scales=w1_plane[a, g][:],
+                in_=grouped[:].rearrange("p t m j -> p (t m j)"),
+            )
+
+        def group_w3(raw):
+            grouped = stage.tile([P, N, PACK], BF16, name="grouped", tag="grouped", align_bytes=64)
+            nc.scalar.copy(
+                out=grouped[:].rearrange("p (c i) j -> p c j i", i=4),
+                in_=raw[:].rearrange("p j (c i) -> p c j i", i=4),
+            )
+            return grouped
+
+        def quantize_w3(grouped, a):
+            nc.vector.quantize_mx(
+                out=w3_codes[a][:].bitcast(FP8X4),
+                scales=w3_plane[a][:],
+                in_=grouped[:].rearrange("p c j -> p (c j)"),
+            )
+
+        def times_v(acc, codes, planes, m_cols, half):
+            cols = slice(half * BANK, (half + 1) * BANK)
+            for a in range(PASSES):
+                nc.tensor.matmul_mx(
+                    out=acc[:],
+                    lhsT=codes[a][:, m_cols].bitcast(FP8X4),
+                    lhsT_scale=planes[a][:, m_cols],
+                    rhs=v_codes[a][:, cols].bitcast(FP8X4),
+                    rhs_scale=v_plane[4 * a : P, cols],
+                    start=(a == 0),
+                    stop=(a == PASSES - 1),
+                )
+
+        olds = {}
+
+        def fetch_old(i):
+            olds[i] = stage.tile([P, S], F32, name="old", tag="old", bufs=3)
+            nc.vector.tensor_copy(out=olds[i][:], in_=pages[i][:].indirect(list2[:]))
+
+        def keep_larger(i):
+            g, t = divmod(i, PACK)
+            for half in range(S // BANK):
+                acc = bank(2 * (i % 2) + half, [P, BANK])
+                times_v(
+                    acc,
+                    [w1_codes[a, g] for a in range(PASSES)],
+                    [w1_plane[a, g] for a in range(PASSES)],
+                    slice(t * P, (t + 1) * P),
+                    half,
+                )
+                cols = slice(half * BANK, (half + 1) * BANK)
+                nc.vector.tensor_tensor(out=olds[i][:, cols], in0=olds[i][:, cols], in1=acc[:], op=MAX)
+
+        def put_back(i):
+            nc.vector.tensor_copy(out=pages[i][:].indirect(list2[:]), in_=olds[i][:])
+
+        def fetch_x(i, first, count):
+            g, t = divmod(i, PACK)
+            nc.vector.tensor_copy(
+                out=x_rows[g][:, t, first : first + count],
+                in_=pages[i][:].indirect(list3[:, first // PER_COLUMN : (first + count) // PER_COLUMN]),
+            )
+
+        def group_x(g, first, count):
+            nc.scalar.copy(
+                out=x_grouped[g][:, first : first + count, :].rearrange("p (c i) t -> p c t i", i=4),
+                in_=x_rows[g][:, :, first : first + count].rearrange("p t (c i) -> p c t i", i=4),
+            )
+
+        def quantize_x(g, first, count):
+            nc.vector.quantize_mx(
+                out=x_codes[g][:, first : first + count].bitcast(FP8X4),
+                scales=x_plane[g][:, first : first + count],
+                in_=x_grouped[g][:, first : first + count, :].rearrange("p c t -> p (c t)"),
+            )
+
+        y_banks = {}
+
+        def score_pass(g, c):
+            cols = slice(c * CHUNK, (c + 1) * CHUNK)
+            if g == 0:
+                y_banks[c] = (bank(2 * c, [P, 2, CHUNK]), bank(2 * c + 1, [P, 1, CHUNK]))
+            for n in range(N_TILES):
+                nc.tensor.matmul_mx(
+                    out=y_banks[c][n // 2][:, n % 2, :],
+                    lhsT=w4_codes[:, g, 2 * P * n : 2 * P * (n + 1)].bitcast(FP4X4),
+                    lhsT_scale=w4_plane[:, g, P * n : P * (n + 1)],
+                    rhs=x_codes[g][:, cols].bitcast(FP8X4),
+                    rhs_scale=x_plane[g][:, cols],
+                    start=(g == 0 and n % 2 == 0),
+                    stop=(g == PASSES - 1 and n > 0),
+                )
+
+        def finish(c):
+            for k, rows in enumerate((slice(0, 2), slice(2, 3))):
+                nc.vector.tensor_tensor(
+                    out=result[:, c, rows, :], in0=result[:, c, rows, :], in1=y_banks[c][k][:], op=MAX
+                )
+            nc.sync.dma_start(
+                out=out[:, c * CHUNK : (c + 1) * CHUNK].rearrange("(n p) j -> p n j", p=P), in_=result[:, c, :, :]
+            )
+
+        nc.vector.memset(tab_plane[:].bitcast(I32), 0)
+        nc.gpsimd.memset(w4_plane[:].rearrange("p a c -> p (a c)").bitcast(I32), 0)
+        nc.sync.dma_start(list1[:], offs)
+        load_tab_codes(0)
+        for q in range(4):
+            nc.sync.dma_start(
+                out=tab_plane[32 * q : 32 * q + 4 * PASSES, :].bitcast(I32),
+                in_=tab_scales[:, 4 * q : 4 * q + 4, :].bitcast(I32),
+            )
+        raw00 = load_w1(0, 0)
+        load_tab_codes(1)
+        nc.sync.dma_start(list2[:], offs2)
+        load_page(0)
+        raw10 = load_w1(1, 0)
+        load_page(1)
+        nc.sync.dma_start(list3[:], offs3)
+
+        nc.vector.tensor_copy(out=v_plane[:], in_=tab_plane[:].indirect(list1[:]))
+        nc.vector.tensor_copy(out=v_codes[0][:], in_=tab_codes[0][:].bitcast(U32).indirect(list1[:]))
+        quantize_w1(group_w1(raw00), 0, 0)
+        nc.vector.tensor_copy(out=v_codes[1][:], in_=tab_codes[1][:].bitcast(U32).indirect(list1[:]))
+        fetch_old(0)
+        quantize_w1(group_w1(raw10), 1, 0)
+
+        raw3 = [load_weight(w3[a * K_PASS : (a + 1) * K_PASS, :]) for a in range(PASSES)]
+        with nc.allow_non_contiguous_dma(reason="one bias value to a partition"):
+            nc.sync.dma_start(out=bias[:], in_=b.rearrange("(n p) -> p n", p=P))
+        nc.sync.dma_start(out=w4_codes[:].bitcast(I32), in_=w4_words.rearrange("a p c -> p a c").bitcast(I32))
+        for q in range(4):
+            nc.sync.dma_start(
+                out=w4_plane[32 * q : 32 * q + 4, :, :].bitcast(I32),
+                in_=w4_scales[:, 4 * q : 4 * q + 4, :].rearrange("a r c -> r a c").bitcast(I32),
+            )
+        load_page(2)
+        load_page(3)
+
+        keep_larger(0)
+        last = PAGE_TILES - 1
+        for i in range(last):
+            fetch_old(i + 1)
+            if i == 0:
+                for a in range(PASSES):
+                    quantize_w3(group_w3(raw3[a]), a)
+                for n in range(N_TILES):
+                    for half in range(S // BANK):
+                        acc = bank(4 + (2 * n + half) % 4, [P, BANK])
+                        times_v(acc, w3_codes, w3_plane, slice(n * P, (n + 1) * P), half)
+                        nc.scalar.activation(
+                            out=result[:, 2 * half : 2 * half + 2, n, :],
+                            in_=acc[:].rearrange("p (c j) -> p c j", j=CHUNK),
+                            func=IDENTITY,
+                            bias=bias[:, n : n + 1],
+                        )
+            if i == 1:
+                for a in range(PASSES):
+                    quantize_w1(group_w1(load_w1(a, 1)), a, 1)
+                for later in range(PACK, PAGE_TILES):
+                    load_page(later)
+            if i == PACK:
+                for half in range(S // BANK):
+                    quantize_x(0, half * BANK, BANK)
+            put_back(i)
+            keep_larger(i + 1)
+            if i < last - 1:
+                fetch_x(i, 0, S)
+            if i == PACK - 1:
+                for half in range(S // BANK):
+                    group_x(0, half * BANK, BANK)
+
+        for c in range(CHUNKS):
+            score_pass(0, c)
+        fetch_x(last - 1, 0, CHUNK)
+        put_back(last)
+        for step in range(CHUNKS + 3):
+            if 0 <= step - 2 < CHUNKS:
+                quantize_x(1, (step - 2) * CHUNK, CHUNK)
+                score_pass(1, step - 2)
+            if 0 <= step - 3 < CHUNKS:
+                finish(step - 3)
+            if step < CHUNKS:
+                if step > 0:
+                    fetch_x(last - 1, step * CHUNK, CHUNK)
+                fetch_x(last, step * CHUNK, CHUNK)
+                group_x(1, step * CHUNK, CHUNK)

@@ -26,6 +26,8 @@ PAGE_TILES = H // P
 CHUNK = 256
 CHUNKS = S // CHUNK
 PER_COLUMN = 16
+ROW_GROUPS = ((0, 2), (256, 2), (512, 4))
+TILES = [(group, t) for group, (first, count) in enumerate(ROW_GROUPS) for t in range(count)]
 
 
 def tile_list_defibrillator_battery_doubt_kernel(
@@ -46,19 +48,22 @@ def tile_list_defibrillator_battery_doubt_kernel(
         list1 = keep.tile([P, S // PER_COLUMN], U16, name="list1")
         list2 = keep.tile([P, S // PER_COLUMN], U16, name="list2")
         list3 = keep.tile([P, S // PER_COLUMN], U16, name="list3")
-        tab_codes = [held("tab_codes%d" % a, [P, T], I32) for a in range(PASSES)]
+        tab_codes = [keep.tile([P, T], I32, name="tab_codes%d" % a, tag="wide%d" % a) for a in range(PASSES)]
         tab_plane = held("tab_plane", [P, T], U8)
         v_codes = [held("v_codes%d" % a, [P, S], U32) for a in range(PASSES)]
         v_plane = held("v_plane", [P, S], U8)
         pages = [held("page%d" % i, [P, T2], F32) for i in range(PAGE_TILES)]
-        w1_codes = {(a, g): held("w1_codes%d%d" % (a, g), [P, K_PASS], U32) for a in range(PASSES) for g in range(PASSES)}
-        w1_plane = {(a, g): held("w1_plane%d%d" % (a, g), [P, K_PASS], U8) for a in range(PASSES) for g in range(PASSES)}
+        w1_codes, w1_plane = {}, {}
+        for group, (first, count) in enumerate(ROW_GROUPS):
+            for a in range(PASSES):
+                w1_codes[a, group] = held("w1_codes%d%d" % (a, group), [P, count * P], U32)
+                w1_plane[a, group] = held("w1_plane%d%d" % (a, group), [P, count * P], U8)
         w3_codes = [held("w3_codes%d" % a, [P, N], U32) for a in range(PASSES)]
         w3_plane = [held("w3_plane%d" % a, [P, N], U8) for a in range(PASSES)]
         w4_codes = held("w4_codes", [P, PASSES, 2 * N], U8)
         w4_plane = held("w4_plane", [P, PASSES, N], U8)
         bias = held("bias", [P, N_TILES], F32)
-        x_rows = [held("x_rows%d" % g, [P, PACK, S], BF16) for g in range(PASSES)]
+        x_rows = {1: held("x_rows1", [P, PACK, S], BF16)}
         x_grouped = [held("x_grouped%d" % g, [P, S, PACK], BF16) for g in range(PASSES)]
         x_codes = [held("x_codes%d" % g, [P, S], U32) for g in range(PASSES)]
         x_plane = [held("x_plane%d" % g, [P, S], U8) for g in range(PASSES)]
@@ -68,42 +73,40 @@ def tile_list_defibrillator_battery_doubt_kernel(
             nc.sync.dma_start(out=tab_codes[a][:], in_=tab_words[a].rearrange("p t i -> p (t i)").bitcast(I32))
 
         def load_page(i):
-            g, t = divmod(i, PACK)
-            rows = page0[g * K_PASS : (g + 1) * K_PASS, :].rearrange("(p t) c -> p t c", t=PACK)
+            group, t = TILES[i]
+            first, count = ROW_GROUPS[group]
+            rows = page0[first : first + count * P, :].rearrange("(p t) c -> p t c", t=count)
             nc.sync.dma_start(out=pages[i][:], in_=rows[:, t, :])
 
-        def load_weight(rows):
-            raw = stage.tile([P, PACK, rows.shape[1]], F32, name="raw", tag="raw", bufs=3)
+        def load_weight(rows, tag):
+            raw = keep.tile([P, PACK, rows.shape[1]], F32, name=tag, tag=tag)
             nc.sync.dma_start(out=raw[:], in_=rows.rearrange("(p j) c -> p j c", j=PACK))
             return raw
 
-        def load_w1(a, g):
-            return load_weight(w1[a * K_PASS : (a + 1) * K_PASS, g * K_PASS : (g + 1) * K_PASS])
+        def load_w1(a, group):
+            first, count = ROW_GROUPS[group]
+            tag = "wide%d" % a if count == PACK else "w1_raw%d%d" % (a, group)
+            return load_weight(w1[a * K_PASS : (a + 1) * K_PASS, first : first + count * P], tag)
 
-        def group_w1(raw):
-            grouped = stage.tile([P, PACK, P, PACK], BF16, name="grouped", tag="grouped", align_bytes=64)
+        def quantize_w1(raw, a, group):
+            count = ROW_GROUPS[group][1]
+            grouped = stage.tile([P, count, P, PACK], BF16, name="grouped", tag="grouped", align_bytes=64)
             nc.scalar.copy(
                 out=grouped[:].rearrange("p t m j -> p m j t"),
-                in_=raw[:].rearrange("p j (m t) -> p m j t", t=PACK),
+                in_=raw[:].rearrange("p j (m t) -> p m j t", t=count),
             )
-            return grouped
-
-        def quantize_w1(grouped, a, g):
             nc.vector.quantize_mx(
-                out=w1_codes[a, g][:].bitcast(FP8X4),
-                scales=w1_plane[a, g][:],
+                out=w1_codes[a, group][:].bitcast(FP8X4),
+                scales=w1_plane[a, group][:],
                 in_=grouped[:].rearrange("p t m j -> p (t m j)"),
             )
 
-        def group_w3(raw):
+        def quantize_w3(raw, a):
             grouped = stage.tile([P, N, PACK], BF16, name="grouped", tag="grouped", align_bytes=64)
             nc.scalar.copy(
                 out=grouped[:].rearrange("p (c i) j -> p c j i", i=4),
                 in_=raw[:].rearrange("p j (c i) -> p c j i", i=4),
             )
-            return grouped
-
-        def quantize_w3(grouped, a):
             nc.vector.quantize_mx(
                 out=w3_codes[a][:].bitcast(FP8X4),
                 scales=w3_plane[a][:],
@@ -123,20 +126,32 @@ def tile_list_defibrillator_battery_doubt_kernel(
                     stop=(a == PASSES - 1),
                 )
 
-        olds = {}
+        def direct_scores():
+            for n in range(N_TILES):
+                for half in range(S // BANK):
+                    acc = bank(4 + (2 * n + half) % 4, [P, BANK])
+                    times_v(acc, w3_codes, w3_plane, slice(n * P, (n + 1) * P), half)
+                    nc.scalar.activation(
+                        out=result[:, 2 * half : 2 * half + 2, n, :],
+                        in_=acc[:].rearrange("p (c j) -> p c j", j=CHUNK),
+                        func=IDENTITY,
+                        bias=bias[:, n : n + 1],
+                    )
+
+        olds, picked = {}, {}
 
         def fetch_old(i):
             olds[i] = stage.tile([P, S], F32, name="old", tag="old", bufs=3)
             nc.vector.tensor_copy(out=olds[i][:], in_=pages[i][:].indirect(list2[:]))
 
         def keep_larger(i):
-            g, t = divmod(i, PACK)
+            group, t = TILES[i]
             for half in range(S // BANK):
                 acc = bank(2 * (i % 2) + half, [P, BANK])
                 times_v(
                     acc,
-                    [w1_codes[a, g] for a in range(PASSES)],
-                    [w1_plane[a, g] for a in range(PASSES)],
+                    [w1_codes[a, group] for a in range(PASSES)],
+                    [w1_plane[a, group] for a in range(PASSES)],
                     slice(t * P, (t + 1) * P),
                     half,
                 )
@@ -146,24 +161,35 @@ def tile_list_defibrillator_battery_doubt_kernel(
         def put_back(i):
             nc.vector.tensor_copy(out=pages[i][:].indirect(list2[:]), in_=olds[i][:])
 
-        def fetch_x(i, first, count):
-            g, t = divmod(i, PACK)
-            nc.vector.tensor_copy(
-                out=x_rows[g][:, t, first : first + count],
-                in_=pages[i][:].indirect(list3[:, first // PER_COLUMN : (first + count) // PER_COLUMN]),
-            )
+        def fetch_x(i):
+            group, t = TILES[i]
+            if i < PACK:
+                tag = "wide1" if i == PACK - 1 else "picked%d" % i
+                picked[i] = keep.tile([P, S], BF16, name="picked%d" % i, tag=tag)
+                nc.vector.tensor_copy(out=picked[i][:], in_=pages[i][:].indirect(list3[:]))
+            else:
+                nc.vector.tensor_copy(out=x_rows[1][:, t, :], in_=pages[i][:].indirect(list3[:]))
 
-        def group_x(g, first, count):
+        def deal_x0():
+            x_rows[0] = keep.tile([P, PACK, S], BF16, name="x_rows0", tag="w3_raw1")
+            for i in range(PACK):
+                group, t = TILES[i]
+                for s in range(2):
+                    nc.sync.dma_start(
+                        out=x_rows[0][64 * group : 64 * (group + 1), 2 * s + t, :], in_=picked[i][s:P:2, :]
+                    )
+
+        def group_x(g, cols, slots):
             nc.scalar.copy(
-                out=x_grouped[g][:, first : first + count, :].rearrange("p (c i) t -> p c t i", i=4),
-                in_=x_rows[g][:, :, first : first + count].rearrange("p t (c i) -> p c t i", i=4),
+                out=x_grouped[g][:, cols, slots].rearrange("p (c i) t -> p c t i", i=4),
+                in_=x_rows[g][:, slots, cols].rearrange("p t (c i) -> p c t i", i=4),
             )
 
-        def quantize_x(g, first, count):
+        def quantize_x(g, cols):
             nc.vector.quantize_mx(
-                out=x_codes[g][:, first : first + count].bitcast(FP8X4),
-                scales=x_plane[g][:, first : first + count],
-                in_=x_grouped[g][:, first : first + count, :].rearrange("p c t -> p (c t)"),
+                out=x_codes[g][:, cols].bitcast(FP8X4),
+                scales=x_plane[g][:, cols],
+                in_=x_grouped[g][:, cols, :].rearrange("p c t -> p (c t)"),
             )
 
         y_banks = {}
@@ -184,15 +210,14 @@ def tile_list_defibrillator_battery_doubt_kernel(
                 )
 
         def finish(c):
+            stored = out[:, c * CHUNK : (c + 1) * CHUNK].rearrange("(n p) j -> p n j", p=P)
             for k, rows in enumerate((slice(0, 2), slice(2, 3))):
                 nc.vector.tensor_tensor(
                     out=result[:, c, rows, :], in0=result[:, c, rows, :], in1=y_banks[c][k][:], op=MAX
                 )
-            nc.sync.dma_start(
-                out=out[:, c * CHUNK : (c + 1) * CHUNK].rearrange("(n p) j -> p n j", p=P), in_=result[:, c, :, :]
-            )
+                nc.sync.dma_start(out=stored[:, rows, :], in_=result[:, c, rows, :])
 
-        nc.vector.memset(tab_plane[:].bitcast(I32), 0)
+        nc.gpsimd.memset(tab_plane[:].bitcast(I32), 0)
         nc.gpsimd.memset(w4_plane[:].rearrange("p a c -> p (a c)").bitcast(I32), 0)
         nc.sync.dma_start(list1[:], offs)
         load_tab_codes(0)
@@ -203,20 +228,24 @@ def tile_list_defibrillator_battery_doubt_kernel(
             )
         raw00 = load_w1(0, 0)
         load_tab_codes(1)
+        raw10 = load_w1(1, 0)
         nc.sync.dma_start(list2[:], offs2)
         load_page(0)
-        raw10 = load_w1(1, 0)
         load_page(1)
         nc.sync.dma_start(list3[:], offs3)
 
-        nc.vector.tensor_copy(out=v_plane[:], in_=tab_plane[:].indirect(list1[:]))
         nc.vector.tensor_copy(out=v_codes[0][:], in_=tab_codes[0][:].bitcast(U32).indirect(list1[:]))
-        quantize_w1(group_w1(raw00), 0, 0)
+        nc.vector.tensor_copy(out=v_plane[:], in_=tab_plane[:].indirect(list1[:]))
+        quantize_w1(raw00, 0, 0)
         nc.vector.tensor_copy(out=v_codes[1][:], in_=tab_codes[1][:].bitcast(U32).indirect(list1[:]))
+        quantize_w1(raw10, 1, 0)
         fetch_old(0)
-        quantize_w1(group_w1(raw10), 1, 0)
+        fetch_old(1)
+        keep_larger(0)
 
-        raw3 = [load_weight(w3[a * K_PASS : (a + 1) * K_PASS, :]) for a in range(PASSES)]
+        w1_raw1 = [load_w1(a, 1) for a in range(PASSES)]
+        load_page(2)
+        w3_raw = [load_weight(w3[a * K_PASS : (a + 1) * K_PASS, :], "w3_raw%d" % a) for a in range(PASSES)]
         with nc.allow_non_contiguous_dma(reason="one bias value to a partition"):
             nc.sync.dma_start(out=bias[:], in_=b.rearrange("(n p) -> p n", p=P))
         nc.sync.dma_start(out=w4_codes[:].bitcast(I32), in_=w4_words.rearrange("a p c -> p a c").bitcast(I32))
@@ -225,54 +254,48 @@ def tile_list_defibrillator_battery_doubt_kernel(
                 out=w4_plane[32 * q : 32 * q + 4, :, :].bitcast(I32),
                 in_=w4_scales[:, 4 * q : 4 * q + 4, :].rearrange("a r c -> r a c").bitcast(I32),
             )
-        load_page(2)
-        load_page(3)
+        for later in range(3, PAGE_TILES):
+            load_page(later)
+        w1_raw2 = [load_w1(a, 2) for a in range(PASSES)]
 
-        keep_larger(0)
+        for a in range(PASSES):
+            quantize_w1(w1_raw1[a], a, 1)
         last = PAGE_TILES - 1
         for i in range(last):
-            fetch_old(i + 1)
-            if i == 0:
-                for a in range(PASSES):
-                    quantize_w3(group_w3(raw3[a]), a)
-                for n in range(N_TILES):
-                    for half in range(S // BANK):
-                        acc = bank(4 + (2 * n + half) % 4, [P, BANK])
-                        times_v(acc, w3_codes, w3_plane, slice(n * P, (n + 1) * P), half)
-                        nc.scalar.activation(
-                            out=result[:, 2 * half : 2 * half + 2, n, :],
-                            in_=acc[:].rearrange("p (c j) -> p c j", j=CHUNK),
-                            func=IDENTITY,
-                            bias=bias[:, n : n + 1],
-                        )
+            if i > 0:
+                fetch_old(i + 1)
             if i == 1:
                 for a in range(PASSES):
-                    quantize_w1(group_w1(load_w1(a, 1)), a, 1)
-                for later in range(PACK, PAGE_TILES):
-                    load_page(later)
-            if i == PACK:
-                for half in range(S // BANK):
-                    quantize_x(0, half * BANK, BANK)
+                    quantize_w3(w3_raw[a], a)
+                direct_scores()
+            if i == PACK - 1:
+                for a in range(PASSES):
+                    quantize_w1(w1_raw2[a], a, 2)
+            if i == PACK + 1:
+                quantize_x(0, slice(0, S))
             put_back(i)
             keep_larger(i + 1)
-            if i < last - 1:
-                fetch_x(i, 0, S)
+            fetch_x(i)
             if i == PACK - 1:
+                deal_x0()
                 for half in range(S // BANK):
-                    group_x(0, half * BANK, BANK)
+                    group_x(0, slice(half * BANK, (half + 1) * BANK), slice(0, PACK))
+            if i == PACK + 1:
+                group_x(1, slice(0, S), slice(0, 2))
 
         for c in range(CHUNKS):
             score_pass(0, c)
-        fetch_x(last - 1, 0, CHUNK)
         put_back(last)
-        for step in range(CHUNKS + 3):
-            if 0 <= step - 2 < CHUNKS:
-                quantize_x(1, (step - 2) * CHUNK, CHUNK)
-                score_pass(1, step - 2)
-            if 0 <= step - 3 < CHUNKS:
-                finish(step - 3)
+        for c in range(CHUNKS):
+            cols = slice(c * CHUNK, (c + 1) * CHUNK)
+            nc.vector.tensor_copy(
+                out=x_rows[1][:, PACK - 1, cols],
+                in_=pages[last][:].indirect(list3[:, cols.start // PER_COLUMN : cols.stop // PER_COLUMN]),
+            )
+            group_x(1, cols, slice(2, PACK))
+        for step in range(CHUNKS + 2):
             if step < CHUNKS:
-                if step > 0:
-                    fetch_x(last - 1, step * CHUNK, CHUNK)
-                fetch_x(last, step * CHUNK, CHUNK)
-                group_x(1, step * CHUNK, CHUNK)
+                quantize_x(1, slice(step * CHUNK, (step + 1) * CHUNK))
+                score_pass(1, step)
+            if step >= 2:
+                finish(step - 2)

from contextlib import ExitStack

import concourse.mybir as mybir

K, T, S, H, N, T2 = 1024, 2048, 1024, 1024, 384, 2048
FLOPS = 2 * K * S * H + 2 * H * S * N + 2 * K * S * N

F32 = mybir.dt.float32
BF16 = mybir.dt.bfloat16
I32 = mybir.dt.int32
U32 = mybir.dt.uint32
U16 = mybir.dt.uint16
U8 = mybir.dt.uint8
FP8X4 = mybir.dt.float8_e4m3fn_x4
FP4X4 = mybir.dt.float4_e2m1fn_x4
MAX = mybir.AluOpType.max
IDENTITY = mybir.ActivationFunctionType.Identity

P = 128
PACK = 4
K_PASS = P * PACK
PASSES = 2
BANK = 512
N_TILES = N // P
PAGE_TILES = H // P
CHUNK = 256
CHUNKS = S // CHUNK
PER_COLUMN = 16
ROW_GROUPS = ((0, 2), (256, 2), (512, 4))
TILES = [(group, t) for group, (first, count) in enumerate(ROW_GROUPS) for t in range(count)]


def tile_list_defibrillator_battery_doubt_kernel(
    tc, tab_words, tab_scales, offs, offs2, offs3, page0, w1, w4_words, w4_scales, w3, b, out
):
    nc = tc.nc
    with ExitStack() as ctx:
        keep = ctx.enter_context(tc.tile_pool(name="keep", bufs=1))
        stage = ctx.enter_context(tc.tile_pool(name="stage", bufs=2))
        psum = ctx.enter_context(tc.psum_pool(name="psum", bufs=1))

        def bank(number, shape):
            return psum.tile(shape, F32, name="bank%d" % number, tag="bank%d" % number)

        def held(name, shape, dtype):
            return keep.tile(shape, dtype, name=name, align_bytes=64)

        list1 = keep.tile([P, S // PER_COLUMN], U16, name="list1")
        list2 = keep.tile([P, S // PER_COLUMN], U16, name="list2")
        list3 = keep.tile([P, S // PER_COLUMN], U16, name="list3")
        tab_codes = [keep.tile([P, T], I32, name="tab_codes%d" % a, tag="wide%d" % a) for a in range(PASSES)]
        tab_plane = held("tab_plane", [P, T], U8)
        v_codes = [held("v_codes%d" % a, [P, S], U32) for a in range(PASSES)]
        v_plane = held("v_plane", [P, S], U8)
        pages = [held("page%d" % i, [P, T2], F32) for i in range(PAGE_TILES)]
        w1_codes, w1_plane = {}, {}
        for group, (first, count) in enumerate(ROW_GROUPS):
            for a in range(PASSES):
                w1_codes[a, group] = held("w1_codes%d%d" % (a, group), [P, count * P], U32)
                w1_plane[a, group] = held("w1_plane%d%d" % (a, group), [P, count * P], U8)
        w3_codes = [held("w3_codes%d" % a, [P, N], U32) for a in range(PASSES)]
        w3_plane = [held("w3_plane%d" % a, [P, N], U8) for a in range(PASSES)]
        w4_codes = held("w4_codes", [P, PASSES, 2 * N], U8)
        w4_plane = held("w4_plane", [P, PASSES, N], U8)
        bias = held("bias", [P, N_TILES], F32)
        x_rows = {1: held("x_rows1", [P, PACK, S], BF16)}
        x_grouped = [held("x_grouped%d" % g, [P, S, PACK], BF16) for g in range(PASSES)]
        x_codes = [held("x_codes%d" % g, [P, S], U32) for g in range(PASSES)]
        x_plane = [held("x_plane%d" % g, [P, S], U8) for g in range(PASSES)]
        result = held("result", [P, CHUNKS, N_TILES, CHUNK], F32)

        def load_tab_codes(a):
            nc.sync.dma_start(out=tab_codes[a][:], in_=tab_words[a].rearrange("p t i -> p (t i)").bitcast(I32))

        def load_page(i):
            group, t = TILES[i]
            first, count = ROW_GROUPS[group]
            rows = page0[first : first + count * P, :].rearrange("(p t) c -> p t c", t=count)
            nc.sync.dma_start(out=pages[i][:], in_=rows[:, t, :])

        def load_weight(rows, tag):
            raw = keep.tile([P, PACK, rows.shape[1]], F32, name=tag, tag=tag)
            nc.sync.dma_start(out=raw[:], in_=rows.rearrange("(p j) c -> p j c", j=PACK))
            return raw

        def load_w1(a, group):
            first, count = ROW_GROUPS[group]
            tag = "wide%d" % a if count == PACK else "w1_raw%d%d" % (a, group)
            return load_weight(w1[a * K_PASS : (a + 1) * K_PASS, first : first + count * P], tag)

        def quantize_w1(raw, a, group):
            count = ROW_GROUPS[group][1]
            grouped = stage.tile([P, count, P, PACK], BF16, name="grouped", tag="grouped", align_bytes=64)
            nc.scalar.copy(
                out=grouped[:].rearrange("p t m j -> p m j t"),
                in_=raw[:].rearrange("p j (m t) -> p m j t", t=count),
            )
            nc.vector.quantize_mx(
                out=w1_codes[a, group][:].bitcast(FP8X4),
                scales=w1_plane[a, group][:],
                in_=grouped[:].rearrange("p t m j -> p (t m j)"),
            )

        def quantize_w3(raw, a):
            grouped = stage.tile([P, N, PACK], BF16, name="grouped", tag="grouped", align_bytes=64)
            nc.scalar.copy(
                out=grouped[:].rearrange("p (c i) j -> p c j i", i=4),
                in_=raw[:].rearrange("p j (c i) -> p c j i", i=4),
            )
            nc.vector.quantize_mx(
                out=w3_codes[a][:].bitcast(FP8X4),
                scales=w3_plane[a][:],
                in_=grouped[:].rearrange("p c j -> p (c j)"),
            )

        def times_v(acc, codes, planes, m_cols, half):
            cols = slice(half * BANK, (half + 1) * BANK)
            for a in range(PASSES):
                nc.tensor.matmul_mx(
                    out=acc[:],
                    lhsT=codes[a][:, m_cols].bitcast(FP8X4),
                    lhsT_scale=planes[a][:, m_cols],
                    rhs=v_codes[a][:, cols].bitcast(FP8X4),
                    rhs_scale=v_plane[4 * a : P, cols],
                    start=(a == 0),
                    stop=(a == PASSES - 1),
                )

        def direct_scores():
            for n in range(N_TILES):
                for half in range(S // BANK):
                    acc = bank(4 + (2 * n + half) % 4, [P, BANK])
                    times_v(acc, w3_codes, w3_plane, slice(n * P, (n + 1) * P), half)
                    nc.scalar.activation(
                        out=result[:, 2 * half : 2 * half + 2, n, :],
                        in_=acc[:].rearrange("p (c j) -> p c j", j=CHUNK),
                        func=IDENTITY,
                        bias=bias[:, n : n + 1],
                    )

        olds, picked = {}, {}

        def fetch_old(i):
            olds[i] = stage.tile([P, S], F32, name="old", tag="old", bufs=3)
            nc.vector.tensor_copy(out=olds[i][:], in_=pages[i][:].indirect(list2[:]))

        def keep_larger(i):
            group, t = TILES[i]
            for half in range(S // BANK):
                acc = bank(2 * (i % 2) + half, [P, BANK])
                times_v(
                    acc,
                    [w1_codes[a, group] for a in range(PASSES)],
                    [w1_plane[a, group] for a in range(PASSES)],
                    slice(t * P, (t + 1) * P),
                    half,
                )
                cols = slice(half * BANK, (half + 1) * BANK)
                nc.vector.tensor_tensor(out=olds[i][:, cols], in0=olds[i][:, cols], in1=acc[:], op=MAX)

        def put_back(i):
            nc.vector.tensor_copy(out=pages[i][:].indirect(list2[:]), in_=olds[i][:])

        def fetch_x(i):
            group, t = TILES[i]
            if i < PACK:
                tag = "wide1" if i == PACK - 1 else "picked%d" % i
                picked[i] = keep.tile([P, S], BF16, name="picked%d" % i, tag=tag)
                nc.vector.tensor_copy(out=picked[i][:], in_=pages[i][:].indirect(list3[:]))
            else:
                nc.vector.tensor_copy(out=x_rows[1][:, t, :], in_=pages[i][:].indirect(list3[:]))

        def deal_x0():
            x_rows[0] = keep.tile([P, PACK, S], BF16, name="x_rows0", tag="w3_raw1")
            for i in range(PACK):
                group, t = TILES[i]
                for s in range(2):
                    nc.sync.dma_start(
                        out=x_rows[0][64 * group : 64 * (group + 1), 2 * s + t, :], in_=picked[i][s:P:2, :]
                    )

        def group_x(g, cols, slots):
            nc.scalar.copy(
                out=x_grouped[g][:, cols, slots].rearrange("p (c i) t -> p c t i", i=4),
                in_=x_rows[g][:, slots, cols].rearrange("p t (c i) -> p c t i", i=4),
            )

        def quantize_x(g, cols):
            nc.vector.quantize_mx(
                out=x_codes[g][:, cols].bitcast(FP8X4),
                scales=x_plane[g][:, cols],
                in_=x_grouped[g][:, cols, :].rearrange("p c t -> p (c t)"),
            )

        y_banks = {}

        def score_pass(g, c):
            cols = slice(c * CHUNK, (c + 1) * CHUNK)
            if g == 0:
                y_banks[c] = (bank(2 * c, [P, 2, CHUNK]), bank(2 * c + 1, [P, 1, CHUNK]))
            for n in range(N_TILES):
                nc.tensor.matmul_mx(
                    out=y_banks[c][n // 2][:, n % 2, :],
                    lhsT=w4_codes[:, g, 2 * P * n : 2 * P * (n + 1)].bitcast(FP4X4),
                    lhsT_scale=w4_plane[:, g, P * n : P * (n + 1)],
                    rhs=x_codes[g][:, cols].bitcast(FP8X4),
                    rhs_scale=x_plane[g][:, cols],
                    start=(g == 0 and n % 2 == 0),
                    stop=(g == PASSES - 1 and n > 0),
                )

        def finish(c):
            stored = out[:, c * CHUNK : (c + 1) * CHUNK].rearrange("(n p) j -> p n j", p=P)
            for k, rows in enumerate((slice(0, 2), slice(2, 3))):
                nc.vector.tensor_tensor(
                    out=result[:, c, rows, :], in0=result[:, c, rows, :], in1=y_banks[c][k][:], op=MAX
                )
                nc.sync.dma_start(out=stored[:, rows, :], in_=result[:, c, rows, :])

        nc.gpsimd.memset(tab_plane[:].bitcast(I32), 0)
        nc.gpsimd.memset(w4_plane[:].rearrange("p a c -> p (a c)").bitcast(I32), 0)
        nc.sync.dma_start(list1[:], offs)
        load_tab_codes(0)
        for q in range(4):
            nc.sync.dma_start(
                out=tab_plane[32 * q : 32 * q + 4 * PASSES, :].bitcast(I32),
                in_=tab_scales[:, 4 * q : 4 * q + 4, :].bitcast(I32),
            )
        raw00 = load_w1(0, 0)
        load_tab_codes(1)
        raw10 = load_w1(1, 0)
        nc.sync.dma_start(list2[:], offs2)
        load_page(0)
        load_page(1)
        nc.sync.dma_start(list3[:], offs3)

        nc.vector.tensor_copy(out=v_codes[0][:], in_=tab_codes[0][:].bitcast(U32).indirect(list1[:]))
        nc.vector.tensor_copy(out=v_plane[:], in_=tab_plane[:].indirect(list1[:]))
        quantize_w1(raw00, 0, 0)
        nc.vector.tensor_copy(out=v_codes[1][:], in_=tab_codes[1][:].bitcast(U32).indirect(list1[:]))
        quantize_w1(raw10, 1, 0)
        fetch_old(0)
        fetch_old(1)
        keep_larger(0)

        w1_raw1 = [load_w1(a, 1) for a in range(PASSES)]
        load_page(2)
        w3_raw = [load_weight(w3[a * K_PASS : (a + 1) * K_PASS, :], "w3_raw%d" % a) for a in range(PASSES)]
        with nc.allow_non_contiguous_dma(reason="one bias value to a partition"):
            nc.sync.dma_start(out=bias[:], in_=b.rearrange("(n p) -> p n", p=P))
        nc.sync.dma_start(out=w4_codes[:].bitcast(I32), in_=w4_words.rearrange("a p c -> p a c").bitcast(I32))
        for q in range(4):
            nc.sync.dma_start(
                out=w4_plane[32 * q : 32 * q + 4, :, :].bitcast(I32),
                in_=w4_scales[:, 4 * q : 4 * q + 4, :].rearrange("a r c -> r a c").bitcast(I32),
            )
        for later in range(3, PAGE_TILES):
            load_page(later)
        w1_raw2 = [load_w1(a, 2) for a in range(PASSES)]

        for a in range(PASSES):
            quantize_w1(w1_raw1[a], a, 1)
        last = PAGE_TILES - 1
        for i in range(last):
            if i > 0:
                fetch_old(i + 1)
            if i == 1:
                for a in range(PASSES):
                    quantize_w3(w3_raw[a], a)
                direct_scores()
            if i == PACK - 1:
                for a in range(PASSES):
                    quantize_w1(w1_raw2[a], a, 2)
            if i == PACK + 1:
                quantize_x(0, slice(0, S))
            put_back(i)
            keep_larger(i + 1)
            fetch_x(i)
            if i == PACK - 1:
                deal_x0()
                for half in range(S // BANK):
                    group_x(0, slice(half * BANK, (half + 1) * BANK), slice(0, PACK))
            if i == PACK + 1:
                group_x(1, slice(0, S), slice(0, 2))

        for c in range(CHUNKS):
            score_pass(0, c)
        put_back(last)
        for c in range(CHUNKS):
            cols = slice(c * CHUNK, (c + 1) * CHUNK)
            nc.vector.tensor_copy(
                out=x_rows[1][:, PACK - 1, cols],
                in_=pages[last][:].indirect(list3[:, cols.start // PER_COLUMN : cols.stop // PER_COLUMN]),
            )
            group_x(1, cols, slice(2, PACK))
        for step in range(CHUNKS + 2):
            if step < CHUNKS:
                quantize_x(1, slice(step * CHUNK, (step + 1) * CHUNK))
                score_pass(1, step)
            if step >= 2:
                finish(step - 2)
